import numpy as np
import ml_dtypes


def mxq(x, axis, fmt="e4m3"):
    dtype, down = {"e4m3": (ml_dtypes.float8_e4m3fn, 7), "e5m2": (ml_dtypes.float8_e5m2, 14)}[fmt]
    v = np.moveaxis(np.asarray(x, np.float32).astype(ml_dtypes.bfloat16).astype(np.float64), axis, -1)
    blocks = v.reshape(v.shape[:-1] + (-1, 32))
    amax = np.abs(blocks).max(-1, keepdims=True)
    byte = np.maximum(np.where(amax > 0, np.frexp(amax)[1] - 1 + 127, 0) - down, 1)
    scale = np.exp2(byte - 127.0)
    codes = (blocks / scale).astype(np.float32).astype(dtype).astype(np.float64)
    return np.moveaxis((codes * scale).reshape(v.shape), -1, axis)


WIDE = False


def mx_kscale(k):
    if not WIDE:
        return np.ones(k)
    levels = np.array([30, -30])
    if k % 512:
        return np.exp2(np.random.permutation(np.resize(levels, k // 32))).repeat(32)
    a = np.empty((k // 512, 16))
    for p in range(k // 512):
        a[p, :8] = np.random.permutation(np.resize(levels, 8))
        for g in range(8):
            far = levels[np.abs(levels - a[p, g]) >= 10]
            a[p, g + 8] = far[np.random.randint(len(far))]
    return np.exp2(a.ravel()).repeat(32)


def f64(x):
    return np.asarray(x).astype(np.float64)


def striped(idx):
    return np.tile(np.asarray(idx).reshape(-1, 16).T, (8, 1)).astype(np.uint16)


def unstriped(offs):
    return offs[:16].T.reshape(-1).astype(np.int64)


E2M1 = np.array([0.0, 0.5, 1.0, 1.5, 2.0, 3.0, 4.0, 6.0, -0.0, -0.5, -1.0, -1.5, -2.0, -3.0, -4.0, -6.0])


def pack_weight(w, fmt):
    k, n = w.shape
    w = f64(np.asarray(w, np.float32).astype(ml_dtypes.bfloat16)).reshape(k // 32, 32, n)
    amax = np.abs(w).max(1)
    if fmt in ("e4m3", "e5m2"):
        byte = np.frexp(amax)[1] - 1 + 127 - (7 if fmt == "e4m3" else 14)
    else:
        mant, ex = np.frexp(amax / 6.0)
        byte = np.where(mant > 0.5, ex, ex - 1) + 127
    byte = np.clip(np.where(amax > 0, byte, 1), 1, 254)
    scaled = (w * np.exp2(127.0 - byte)[:, None, :]).reshape(k, n).astype(np.float32)
    by_word = np.ascontiguousarray(scaled.reshape(k // 512, 128, 4, n).transpose(0, 1, 3, 2))
    if fmt in ("e4m3", "e5m2"):
        words = by_word.astype(ml_dtypes.float8_e4m3fn if fmt == "e4m3" else ml_dtypes.float8_e5m2).view(np.uint8)
    else:
        c = by_word.astype(ml_dtypes.float4_e2m1fn).view(np.uint8) & 0xF
        words = (c[..., 0::2] | (c[..., 1::2] << 4)).reshape(k // 512, 128, 2 * n)
    return np.ascontiguousarray(words), np.ascontiguousarray(byte.astype(np.uint8).reshape(k // 512, 16, n))


def unpack_weight(words, scales, fmt):
    g, _, n = scales.shape
    words = np.ascontiguousarray(words).reshape(g, 128, n, -1)
    if fmt in ("e4m3", "e5m2"):
        vals = words.view(ml_dtypes.float8_e4m3fn if fmt == "e4m3" else ml_dtypes.float8_e5m2).astype(np.float64)
    else:
        nib = np.empty((g, 128, n, 4), np.uint8)
        nib[..., 0::2] = words & 0xF
        nib[..., 1::2] = words >> 4
        vals = E2M1[nib]
    vals = vals * np.repeat(np.exp2(scales.astype(np.float64) - 127.0), 8, axis=1)[..., None]
    return vals.transpose(0, 1, 3, 2).reshape(g * 512, n)


K, T, J, I, L, S, R, X, N, Z = 1024, 1024, 256, 128, 128, 512, 512, 512, 256, 512


def setup_inputs():
    n = np.random.standard_normal
    idx = np.random.permutation(T)[:I]
    idx2 = np.random.permutation(S)[:L]
    idx3 = np.random.permutation(Z)[:J]
    fk = mx_kscale(K)
    fr = mx_kscale(R)
    fx = mx_kscale(X)
    sxp = pack_weight(n((X, J)) / fx[:, None], "e5m2")
    wsp = pack_weight(n((X, R)) * 1 / np.sqrt(X) * fx[:, None] * fr, "e5m2")
    wbp = pack_weight(n((R, N)) * 1 / np.sqrt(R) / fr[:, None], "e2m1")
    return {
        "xa": (n((K, T)) / fk[:, None]).astype(np.float32),
        "xb": (n((K, S)) * 0.6 / fk[:, None]).astype(np.float32),
        "w": (n((K, R)) * 1 / np.sqrt(K) * fk[:, None] * fr).astype(np.float32),
        "sx_words": sxp[0],
        "sx_scales": sxp[1],
        "ws_words": wsp[0],
        "ws_scales": wsp[1],
        "wb_words": wbp[0],
        "wb_scales": wbp[1],
        "tz": (n((N, Z)) * 0.6).astype(np.float32),
        "rw": (np.random.uniform(0.5, 2.0, (1, J))).astype(np.float32),
        "offs": striped(idx),
        "offs2": striped(idx2),
        "offs3": striped(idx3),
    }


def reference(xa, xb, w, sx_words, sx_scales, ws_words, ws_scales, wb_words, wb_scales, tz, rw, offs, offs2, offs3):
    idx = unstriped(offs)
    idx2 = unstriped(offs2)
    idx3 = unstriped(offs3)
    sxu = unpack_weight(sx_words, sx_scales, "e5m2")
    wsu = unpack_weight(ws_words, ws_scales, "e5m2")
    wbu = unpack_weight(wb_words, wb_scales, "e2m1")
    u = np.concatenate([f64(xa)[:, idx], f64(xb)[:, idx2]], axis=1)
    wq = mxq(f64(w), 0, "e5m2")
    uq = mxq(u, 0, "e4m3")
    a = wq.T @ uq
    b2 = wsu.T @ sxu
    hid = np.maximum(a, b2)
    hidq = mxq(hid, 0, "e5m2")
    p = wbu.T @ hidq
    y = np.maximum(p, f64(tz)[:, idx3]) * f64(rw)
    return y

@@ -1,0 +1,229 @@
+from contextlib import ExitStack
+
+import concourse.mybir as mybir
+from concourse.masks import make_identity
+
+K, T, J, S, R, X, N, Z = 1024, 1024, 256, 512, 512, 512, 256, 512
+FLOPS = 2 * J * (K * R + X * R + R * N)
+
+F32 = mybir.dt.float32
+BF16 = mybir.dt.bfloat16
+I32 = mybir.dt.int32
+U32 = mybir.dt.uint32
+U16 = mybir.dt.uint16
+U8 = mybir.dt.uint8
+E4M3 = mybir.dt.float8_e4m3fn_x4
+E5M2 = mybir.dt.float8_e5m2_x4
+E2M1 = mybir.dt.float4_e2m1fn_x4
+MAX = mybir.AluOpType.max
+MULT = mybir.AluOpType.mult
+COPY = mybir.ActivationFunctionType.Copy
+
+P = 128
+PACK = 4
+K_PASS = P * PACK
+PASSES = K // K_PASS
+HALF = J // 2
+N_TILES = N // P
+LIST_COLS = HALF // 16
+XA, XB = 0, 1
+
+
+def tile_list_joined_rival_floored_kernel(
+    tc, xa, xb, w, sx_words, sx_scales, ws_words, ws_scales, wb_words, wb_scales, tz, rw, offs, offs2, offs3, out
+):
+    nc = tc.nc
+    with ExitStack() as ctx:
+        lists = ctx.enter_context(tc.tile_pool(name="lists", bufs=1))
+        sb = ctx.enter_context(tc.tile_pool(name="sb", bufs=1))
+        ps = ctx.enter_context(tc.psum_pool(name="ps", bufs=1))
+
+        def tile(name, shape, dtype):
+            return sb.tile(shape, dtype, name=name, align_bytes=64)
+
+        def pass_rows(table, a):
+            return table[a * K_PASS : (a + 1) * K_PASS, :].rearrange("(p i) c -> p i c", i=PACK)
+
+        def load_planes(name, table, a, first, count):
+            raw = tile(name, [P, count, table.shape[1]], F32)
+            nc.sync.dma_start(out=raw[:], in_=pass_rows(table, a)[:, first : first + count, :])
+            return [raw[:, i, :] for i in range(count)], raw
+
+        def load_list(name, src):
+            dst = lists.tile(list(src.shape), U16, name=name)
+            nc.sync.dma_start(dst[:], src)
+            return dst
+
+        def load_words(name, src, dtype, width):
+            dst = tile(name, [P, width], dtype)
+            nc.sync.dma_start(out=dst[:].bitcast(I32), in_=src.bitcast(I32))
+            return dst
+
+        given_scales = tile("given_scales", [P, R + J + N], U8)
+        nc.vector.memset(given_scales[:].bitcast(U32), 0)
+        ws_scale_raw = given_scales[:, 0:R]
+        sx_scale = given_scales[:, R : R + J]
+        wb_scale = given_scales[:, R + J : R + J + N]
+
+        def load_scales(dst, src):
+            for q in range(4):
+                nc.sync.dma_start(
+                    out=dst[32 * q : 32 * q + 4, :].bitcast(I32), in_=src[0, 4 * q : 4 * q + 4, :].bitcast(I32)
+                )
+
+        rw_rows = tile("rw_rows", [P, P], F32)
+        nc.vector.memset(rw_rows[:], 0.0)
+        ident = tile("ident", [P, P], F32)
+        make_identity(nc, ident[:])
+
+        windows = {}
+        w_raw = {}
+        windows[XB, 0], unused = load_planes("xb0", xb, 0, 0, PACK)
+        offsets = {XB: load_list("offs2", offs2)}
+        unused, w_raw[0] = load_planes("w0", w, 0, 0, PACK)
+        offsets[XA] = load_list("offs", offs)
+        tz_offsets = load_list("offs3", offs3)
+        nc.sync.dma_start(out=rw_rows[0:2, :], in_=rw.rearrange("o (h c) -> (o h) c", h=2))
+        windows[XB, 1], unused = load_planes("xb1", xb, 1, 0, PACK)
+        load_scales(ws_scale_raw, ws_scales)
+        unused, w_raw[1] = load_planes("w1", w, 1, 0, PACK)
+        ws_raw = load_words("ws_raw", ws_words[0].rearrange("p c t -> p (c t)"), U32, R)
+        load_scales(sx_scale, sx_scales)
+        sx_codes = load_words("sx_codes", sx_words[0].rearrange("p c t -> p (c t)"), U32, J)
+        windows[XA, 0], unused = load_planes("xa0", xa, 0, 0, PACK)
+        load_scales(wb_scale, wb_scales)
+        wb_codes = load_words("wb_codes", wb_words[0], U8, 2 * N)
+        first, unused = load_planes("xa1_01", xa, 1, 0, 2)
+        second, unused = load_planes("xa1_2", xa, 1, 2, 1)
+        third, unused = load_planes("xa1_3", xa, 1, 3, 1)
+        windows[XA, 1] = first + second + third
+        tz_raw = []
+        for nt in range(N_TILES):
+            raw = tile("tz%d" % nt, [P, Z], F32)
+            nc.sync.dma_start(out=raw[:], in_=tz[nt * P : (nt + 1) * P, :])
+            tz_raw.append(raw)
+
+        rw_bank = ps.tile([P, 3, P], F32, name="rw_bank")
+        nc.tensor.transpose(rw_bank[:, 2, :], rw_rows[:], ident[:])
+        rw_cols = tile("rw_cols", [P, 2], F32)
+        nc.scalar.copy(out=rw_cols[:], in_=rw_bank[:, 2, 0:2])
+        for h in range(2):
+            nc.tensor.transpose(rw_bank[:, h, :], rw_cols[:, h : h + 1].to_broadcast([P, P]), ident[:])
+        rw_all = tile("rw_all", [P, 2, P], F32)
+        nc.scalar.copy(out=rw_all[:], in_=rw_bank[:, 0:2, :])
+
+        def quantise(name, values, fmt):
+            width = values.shape[1] // PACK
+            codes = tile(name + "_codes", [P, width], U32)
+            scales = tile(name + "_scales", [P, width], U8)
+            nc.vector.quantize_mx(out=codes[:].bitcast(fmt), scales=scales[:], in_=values)
+            return codes, scales
+
+        def quantise_w(a):
+            rounded = tile("w_bf%d" % a, [P, R * PACK], BF16)
+            nc.scalar.copy(
+                out=rounded[:].rearrange("p (t m i) -> p m t i", t=PACK, i=PACK),
+                in_=w_raw[a][:].rearrange("p i (m t) -> p m t i", t=PACK),
+            )
+            return quantise("w%d" % a, rounded[:], E5M2)
+
+        def quantise_u(h, a):
+            rounded = tile("u_bf%d%d" % (h, a), [P, HALF, PACK], BF16)
+            for i in range(PACK):
+                nc.vector.tensor_copy(out=rounded[:, :, i], in_=windows[h, a][i].indirect(offsets[h][:]))
+            return quantise("u%d%d" % (h, a), rounded[:].rearrange("p j i -> p (j i)"), E4M3)
+
+        a_bank = [ps.tile([P, PACK, HALF], F32, name="a_bank%d" % h) for h in range(2)]
+
+        def first_product(h, a, wq, uq):
+            for t in range(PACK):
+                cols = slice(t * P, (t + 1) * P)
+                nc.tensor.matmul_mx(
+                    out=a_bank[h][:, t, :],
+                    lhsT=wq[0][:, cols].bitcast(E5M2),
+                    lhsT_scale=wq[1][:, cols],
+                    rhs=uq[0][:].bitcast(E4M3),
+                    rhs_scale=uq[1][:],
+                    start=(a == 0 and t == 0),
+                    stop=(a == PASSES - 1 and t == PACK - 1),
+                )
+
+        def rival(h, ws_codes, ws_scale):
+            bank = ps.tile([P, PACK, HALF], F32, name="b2_bank%d" % h)
+            slots = slice(h * HALF, (h + 1) * HALF)
+            for t in range(PACK):
+                cols = slice(t * P, (t + 1) * P)
+                nc.tensor.matmul_mx(
+                    out=bank[:, t, :],
+                    lhsT=ws_codes[:, cols].bitcast(E5M2),
+                    lhsT_scale=ws_scale[:, cols],
+                    rhs=sx_codes[:, slots].bitcast(E5M2),
+                    rhs_scale=sx_scale[:, slots],
+                    start=True,
+                    stop=True,
+                )
+            b2 = tile("b2_%d" % h, [P, HALF, PACK], F32)
+            nc.scalar.copy(out=b2[:], in_=bank[:].rearrange("p t j -> p j t"))
+            return b2
+
+        def second_product(h, b2, banks):
+            hid = tile("hid%d" % h, [P, HALF, PACK], BF16)
+            nc.vector.tensor_tensor(out=hid[:], in0=a_bank[h][:].rearrange("p t j -> p j t"), in1=b2[:], op=MAX)
+            codes, scales = quantise("hid%d" % h, hid[:].rearrange("p j t -> p (j t)"), E5M2)
+            for nt in range(N_TILES):
+                nc.tensor.matmul_mx(
+                    out=banks[nt],
+                    lhsT=wb_codes[:, 2 * nt * P : 2 * (nt + 1) * P].bitcast(E2M1),
+                    lhsT_scale=wb_scale[:, nt * P : (nt + 1) * P],
+                    rhs=codes[:].bitcast(E5M2),
+                    rhs_scale=scales[:],
+                    start=True,
+                    stop=True,
+                )
+
+        def gather_tz(h, nt):
+            picked = tile("tz_picked%d%d" % (h, nt), [P, HALF], F32)
+            cols = tz_offsets[:, h * LIST_COLS : (h + 1) * LIST_COLS]
+            nc.scalar.activation(picked[:], tz_raw[nt][:].indirect(cols), COPY)
+            return picked
+
+        def floor(h, nt, bank, picked):
+            floored = tile("floored%d%d" % (h, nt), [P, HALF], F32)
+            nc.vector.tensor_tensor(out=floored[:], in0=bank, in1=picked[:], op=MAX)
+            return floored
+
+        def weigh_and_store(h, nt, floored):
+            y = tile("y%d%d" % (h, nt), [P, HALF], F32)
+            nc.vector.tensor_tensor(out=y[:], in0=floored[:], in1=rw_all[:, h, :], op=MULT)
+            nc.sync.dma_start(out=out[nt * P : (nt + 1) * P, h * HALF : (h + 1) * HALF], in_=y[:])
+
+        p_xb = ps.tile([P, N_TILES, HALF], F32, name="p_xb")
+        p_xa = [ps.tile([P, HALF], F32, name="p_xa%d" % nt) for nt in range(N_TILES)]
+        p_banks = {XB: [p_xb[:, nt, :] for nt in range(N_TILES)], XA: [b[:] for b in p_xa]}
+
+        wq = {}
+        uq = quantise_u(XB, 0)
+        wq[0] = quantise_w(0)
+        first_product(XB, 0, wq[0], uq)
+        uq = quantise_u(XB, 1)
+        ws_codes = tile("ws_codes", [P, R], U32)
+        ws_scale = tile("ws_scale", [P, R], U8)
+        nc.vector.tensor_copy(
+            out=ws_scale[:].rearrange("p (t m) -> p t m", t=PACK), in_=ws_scale_raw.rearrange("p (m t) -> p t m", t=PACK)
+        )
+        nc.vector.tensor_copy(
+            out=ws_codes[:].rearrange("p (t m) -> p t m", t=PACK), in_=ws_raw[:].rearrange("p (m t) -> p t m", t=PACK)
+        )
+        wq[1] = quantise_w(1)
+        b2 = {h: rival(h, ws_codes, ws_scale) for h in (XB, XA)}
+        first_product(XB, 1, wq[1], uq)
+        second_product(XB, b2[XB], p_banks[XB])
+        for a in range(PASSES):
+            first_product(XA, a, wq[a], quantise_u(XA, a))
+        picked = {(h, nt): gather_tz(h, nt) for h, nt in ((XB, 0), (XA, 0), (XB, 1), (XA, 1))}
+        weigh_and_store(XB, 0, floor(XB, 0, p_banks[XB][0], picked[XB, 0]))
+        second_product(XA, b2[XA], p_banks[XA])
+        weigh_and_store(XB, 1, floor(XB, 1, p_banks[XB][1], picked[XB, 1]))
+        floored = [floor(XA, nt, p_banks[XA][nt], picked[XA, nt]) for nt in range(N_TILES)]
+        for nt in range(N_TILES):
+            weigh_and_store(XA, nt, floored[nt])

@@ -27,6 +27,7 @@ HALF = J // 2
 N_TILES = N // P
 LIST_COLS = HALF // 16
 XA, XB = 0, 1
+W_SPLIT = 64
 
 
 def tile_list_joined_rival_floored_kernel(
@@ -59,17 +60,23 @@ def tile_list_joined_rival_floored_kernel(
             nc.sync.dma_start(out=dst[:].bitcast(I32), in_=src.bitcast(I32))
             return dst
 
-        given_scales = tile("given_scales", [P, R + J + N], U8)
-        nc.vector.memset(given_scales[:].bitcast(U32), 0)
+        staged = tile("staged_scales", [P, 4, R + J + N], U8)
+        given_scales = staged[:, 0, :]
+        nc.vector.memset(given_scales.bitcast(U32), 0)
         ws_scale_raw = given_scales[:, 0:R]
         sx_scale = given_scales[:, R : R + J]
         wb_scale = given_scales[:, R + J : R + J + N]
 
-        def load_scales(dst, src):
-            for q in range(4):
-                nc.sync.dma_start(
-                    out=dst[32 * q : 32 * q + 4, :].bitcast(I32), in_=src[0, 4 * q : 4 * q + 4, :].bitcast(I32)
-                )
+        def load_scales(src, first):
+            width = src.shape[2]
+            nc.sync.dma_start(
+                out=staged[0:P:32, :, first : first + width].bitcast(I32),
+                in_=src[0].rearrange("(q r) c -> q r c", r=4).bitcast(I32),
+            )
+
+        def deal_scales():
+            for r in range(1, 4):
+                nc.sync.dma_start(out=staged[r:P:32, 0, :].bitcast(I32), in_=staged[0:P:32, r, :].bitcast(I32))
 
         rw_rows = tile("rw_rows", [P, P], F32)
         nc.vector.memset(rw_rows[:], 0.0)
@@ -78,25 +85,28 @@ def tile_list_joined_rival_floored_kernel(
 
         windows = {}
         w_raw = {}
-        windows[XB, 0], unused = load_planes("xb0", xb, 0, 0, PACK)
+        xb_raw = tile("xb", [P, PASSES, PACK * S], F32)
+        nc.sync.dma_start(out=xb_raw[:], in_=xb.rearrange("(a p i) c -> p a (i c)", a=PASSES, i=PACK))
+        for a in range(PASSES):
+            windows[XB, a] = [xb_raw[:, a, i * S : (i + 1) * S] for i in range(PACK)]
         offsets = {XB: load_list("offs2", offs2)}
+        load_scales(ws_scales, 0)
+        load_scales(sx_scales, R)
+        load_scales(wb_scales, R + J)
         unused, w_raw[0] = load_planes("w0", w, 0, 0, PACK)
-        offsets[XA] = load_list("offs", offs)
-        tz_offsets = load_list("offs3", offs3)
         nc.sync.dma_start(out=rw_rows[0:2, :], in_=rw.rearrange("o (h c) -> (o h) c", h=2))
-        windows[XB, 1], unused = load_planes("xb1", xb, 1, 0, PACK)
-        load_scales(ws_scale_raw, ws_scales)
         unused, w_raw[1] = load_planes("w1", w, 1, 0, PACK)
         ws_raw = load_words("ws_raw", ws_words[0].rearrange("p c t -> p (c t)"), U32, R)
-        load_scales(sx_scale, sx_scales)
+        deal_scales()
         sx_codes = load_words("sx_codes", sx_words[0].rearrange("p c t -> p (c t)"), U32, J)
         windows[XA, 0], unused = load_planes("xa0", xa, 0, 0, PACK)
-        load_scales(wb_scale, wb_scales)
+        offsets[XA] = load_list("offs", offs)
         wb_codes = load_words("wb_codes", wb_words[0], U8, 2 * N)
         first, unused = load_planes("xa1_01", xa, 1, 0, 2)
         second, unused = load_planes("xa1_2", xa, 1, 2, 1)
         third, unused = load_planes("xa1_3", xa, 1, 3, 1)
         windows[XA, 1] = first + second + third
+        tz_offsets = load_list("offs3", offs3)
         tz_raw = []
         for nt in range(N_TILES):
             raw = tile("tz%d" % nt, [P, Z], F32)
@@ -121,16 +131,22 @@ def tile_list_joined_rival_floored_kernel(
 
         def quantise_w(a):
             rounded = tile("w_bf%d" % a, [P, R * PACK], BF16)
-            nc.scalar.copy(
-                out=rounded[:].rearrange("p (t m i) -> p m t i", t=PACK, i=PACK),
-                in_=w_raw[a][:].rearrange("p i (m t) -> p m t i", t=PACK),
-            )
+            dealt = rounded[:].rearrange("p (t m i) -> p m t i", t=PACK, i=PACK)
+            source = w_raw[a][:].rearrange("p i (m t) -> p m t i", t=PACK)
+            nc.scalar.copy(out=dealt[:, :W_SPLIT], in_=source[:, :W_SPLIT])
+            nc.vector.tensor_copy(out=dealt[:, W_SPLIT:], in_=source[:, W_SPLIT:])
             return quantise("w%d" % a, rounded[:], E5M2)
 
         def quantise_u(h, a):
             rounded = tile("u_bf%d%d" % (h, a), [P, HALF, PACK], BF16)
-            for i in range(PACK):
-                nc.vector.tensor_copy(out=rounded[:, :, i], in_=windows[h, a][i].indirect(offsets[h][:]))
+            if (h, a) == (XA, 0):
+                picked = tile("u_picked", [P, PACK, HALF], F32)
+                for i in range(PACK):
+                    nc.scalar.activation(picked[:, i, :], windows[h, a][i].indirect(offsets[h][:]), COPY)
+                nc.vector.tensor_copy(out=rounded[:], in_=picked[:].rearrange("p i j -> p j i"))
+            else:
+                for i in range(PACK):
+                    nc.vector.tensor_copy(out=rounded[:, :, i], in_=windows[h, a][i].indirect(offsets[h][:]))
             return quantise("u%d%d" % (h, a), rounded[:].rearrange("p j i -> p (j i)"), E4M3)
 
         a_bank = [ps.tile([P, PACK, HALF], F32, name="a_bank%d" % h) for h in range(2)]
@@ -195,17 +211,18 @@ def tile_list_joined_rival_floored_kernel(
         def weigh_and_store(h, nt, floored):
             y = tile("y%d%d" % (h, nt), [P, HALF], F32)
             nc.vector.tensor_tensor(out=y[:], in0=floored[:], in1=rw_all[:, h, :], op=MULT)
-            nc.sync.dma_start(out=out[nt * P : (nt + 1) * P, h * HALF : (h + 1) * HALF], in_=y[:])
+            queue = nc.scalar if nt == 1 else nc.sync
+            queue.dma_start(out=out[nt * P : (nt + 1) * P, h * HALF : (h + 1) * HALF], in_=y[:])
 
         p_xb = ps.tile([P, N_TILES, HALF], F32, name="p_xb")
         p_xa = [ps.tile([P, HALF], F32, name="p_xa%d" % nt) for nt in range(N_TILES)]
         p_banks = {XB: [p_xb[:, nt, :] for nt in range(N_TILES)], XA: [b[:] for b in p_xa]}
 
         wq = {}
-        uq = quantise_u(XB, 0)
-        wq[0] = quantise_w(0)
-        first_product(XB, 0, wq[0], uq)
+        uq0 = quantise_u(XB, 0)
         uq = quantise_u(XB, 1)
+        wq[0] = quantise_w(0)
+        first_product(XB, 0, wq[0], uq0)
         ws_codes = tile("ws_codes", [P, R], U32)
         ws_scale = tile("ws_scale", [P, R], U8)
         nc.vector.tensor_copy(

@@ -39,8 +39,8 @@ def tile_list_joined_rival_floored_kernel(
         sb = ctx.enter_context(tc.tile_pool(name="sb", bufs=1))
         ps = ctx.enter_context(tc.psum_pool(name="ps", bufs=1))
 
-        def tile(name, shape, dtype):
-            return sb.tile(shape, dtype, name=name, align_bytes=64)
+        def tile(name, shape, dtype, tag=None):
+            return sb.tile(shape, dtype, name=name, tag=tag or name, align_bytes=64)
 
         def pass_rows(table, a):
             return table[a * K_PASS : (a + 1) * K_PASS, :].rearrange("(p i) c -> p i c", i=PACK)
@@ -98,14 +98,16 @@ def tile_list_joined_rival_floored_kernel(
         unused, w_raw[1] = load_planes("w1", w, 1, 0, PACK)
         ws_raw = load_words("ws_raw", ws_words[0].rearrange("p c t -> p (c t)"), U32, R)
         deal_scales()
-        sx_codes = load_words("sx_codes", sx_words[0].rearrange("p c t -> p (c t)"), U32, J)
+        sx_rows = sx_words[0].rearrange("p c t -> p (c t)")
+        sx_codes = {XB: load_words("sx_codes1", sx_rows[:, PACK * HALF :], U32, HALF)}
         windows[XA, 0], unused = load_planes("xa0", xa, 0, 0, PACK)
         offsets[XA] = load_list("offs", offs)
-        wb_codes = load_words("wb_codes", wb_words[0], U8, 2 * N)
         first, unused = load_planes("xa1_01", xa, 1, 0, 2)
+        sx_codes[XA] = load_words("sx_codes0", sx_rows[:, : PACK * HALF], U32, HALF)
         second, unused = load_planes("xa1_2", xa, 1, 2, 1)
         third, unused = load_planes("xa1_3", xa, 1, 3, 1)
         windows[XA, 1] = first + second + third
+        wb_codes = load_words("wb_codes", wb_words[0], U8, 2 * N)
         tz_offsets = load_list("offs3", offs3)
         tz_raw = []
         for nt in range(N_TILES):
@@ -173,7 +175,7 @@ def tile_list_joined_rival_floored_kernel(
                     out=bank[:, t, :],
                     lhsT=ws_codes[:, cols].bitcast(E5M2),
                     lhsT_scale=ws_scale[:, cols],
-                    rhs=sx_codes[:, slots].bitcast(E5M2),
+                    rhs=sx_codes[h][:].bitcast(E5M2),
                     rhs_scale=sx_scale[:, slots],
                     start=True,
                     stop=True,
@@ -182,10 +184,13 @@ def tile_list_joined_rival_floored_kernel(
             nc.scalar.copy(out=b2[:], in_=bank[:].rearrange("p t j -> p j t"))
             return b2
 
-        def second_product(h, b2, banks):
+        def larger(h, b2):
             hid = tile("hid%d" % h, [P, HALF, PACK], BF16)
             nc.vector.tensor_tensor(out=hid[:], in0=a_bank[h][:].rearrange("p t j -> p j t"), in1=b2[:], op=MAX)
-            codes, scales = quantise("hid%d" % h, hid[:].rearrange("p j t -> p (j t)"), E5M2)
+            return quantise("hid%d" % h, hid[:].rearrange("p j t -> p (j t)"), E5M2)
+
+        def second_product(hid, banks):
+            codes, scales = hid
             for nt in range(N_TILES):
                 nc.tensor.matmul_mx(
                     out=banks[nt],
@@ -197,22 +202,12 @@ def tile_list_joined_rival_floored_kernel(
                     stop=True,
                 )
 
-        def gather_tz(h, nt):
-            picked = tile("tz_picked%d%d" % (h, nt), [P, HALF], F32)
+        def gather_tz(h):
+            picked = tile("tz_picked%d" % h, [P, N_TILES, HALF], F32, tag="picked_then_floored" if h == XB else None)
             cols = tz_offsets[:, h * LIST_COLS : (h + 1) * LIST_COLS]
-            nc.scalar.activation(picked[:], tz_raw[nt][:].indirect(cols), COPY)
+            for nt in range(N_TILES):
+                nc.scalar.activation(picked[:, nt, :], tz_raw[nt][:].indirect(cols), COPY)
             return picked
-
-        def floor(h, nt, bank, picked):
-            floored = tile("floored%d%d" % (h, nt), [P, HALF], F32)
-            nc.vector.tensor_tensor(out=floored[:], in0=bank, in1=picked[:], op=MAX)
-            return floored
-
-        def weigh_and_store(h, nt, floored):
-            y = tile("y%d%d" % (h, nt), [P, HALF], F32)
-            nc.vector.tensor_tensor(out=y[:], in0=floored[:], in1=rw_all[:, h, :], op=MULT)
-            queue = nc.scalar if nt == 1 else nc.sync
-            queue.dma_start(out=out[nt * P : (nt + 1) * P, h * HALF : (h + 1) * HALF], in_=y[:])
 
         p_xb = ps.tile([P, N_TILES, HALF], F32, name="p_xb")
         p_xa = [ps.tile([P, HALF], F32, name="p_xa%d" % nt) for nt in range(N_TILES)]
@@ -232,15 +227,28 @@ def tile_list_joined_rival_floored_kernel(
             out=ws_codes[:].rearrange("p (t m) -> p t m", t=PACK), in_=ws_raw[:].rearrange("p (m t) -> p t m", t=PACK)
         )
         wq[1] = quantise_w(1)
-        b2 = {h: rival(h, ws_codes, ws_scale) for h in (XB, XA)}
+        b2 = {XB: rival(XB, ws_codes, ws_scale)}
         first_product(XB, 1, wq[1], uq)
-        second_product(XB, b2[XB], p_banks[XB])
-        for a in range(PASSES):
-            first_product(XA, a, wq[a], quantise_u(XA, a))
-        picked = {(h, nt): gather_tz(h, nt) for h, nt in ((XB, 0), (XA, 0), (XB, 1), (XA, 1))}
-        weigh_and_store(XB, 0, floor(XB, 0, p_banks[XB][0], picked[XB, 0]))
-        second_product(XA, b2[XA], p_banks[XA])
-        weigh_and_store(XB, 1, floor(XB, 1, p_banks[XB][1], picked[XB, 1]))
-        floored = [floor(XA, nt, p_banks[XA][nt], picked[XA, nt]) for nt in range(N_TILES)]
+        hid_xb = larger(XB, b2[XB])
+        first_product(XA, 0, wq[0], quantise_u(XA, 0))
+        b2[XA] = rival(XA, ws_codes, ws_scale)
+        second_product(hid_xb, p_banks[XB])
+        first_product(XA, 1, wq[1], quantise_u(XA, 1))
+        picked = {h: gather_tz(h) for h in (XB, XA)}
+        second_product(larger(XA, b2[XA]), p_banks[XA])
+        out_tiles = out.rearrange("(nt p) (h j) -> p nt h j", p=P, j=HALF)
+
+        floored = tile("floored_xb", [P, N_TILES, HALF], F32)
+        nc.vector.tensor_tensor(out=floored[:], in0=p_xb[:], in1=picked[XB][:], op=MAX)
+        y = tile("y_xb", [P, N_TILES, HALF], F32)
+        weights = rw_all[:, XB : XB + 1, :].to_broadcast([P, N_TILES, HALF])
+        nc.vector.tensor_tensor(out=y[:], in0=floored[:], in1=weights, op=MULT)
+        nc.sync.dma_start(out=out_tiles[:, :, XB, :], in_=y[:])
+
+        floored = tile("floored_xa", [P, N_TILES, HALF], F32, tag="picked_then_floored")
         for nt in range(N_TILES):
-            weigh_and_store(XA, nt, floored[nt])
+            nc.vector.tensor_tensor(out=floored[:, nt, :], in0=p_banks[XA][nt], in1=picked[XA][:, nt, :], op=MAX)
+        for nt, queue in enumerate((nc.sync, nc.scalar)):
+            y = tile("y_xa%d" % nt, [P, HALF], F32)
+            nc.vector.tensor_tensor(out=y[:], in0=floored[:, nt, :], in1=rw_all[:, XA, :], op=MULT)
+            queue.dma_start(out=out_tiles[:, nt, XA, :], in_=y[:])

from contextlib import ExitStack

import concourse.mybir as mybir
from concourse.masks import make_identity

K, T, J, S, R, X, N, Z = 1024, 1024, 256, 512, 512, 512, 256, 512
FLOPS = 2 * J * (K * R + X * R + R * N)

F32 = mybir.dt.float32
BF16 = mybir.dt.bfloat16
I32 = mybir.dt.int32
U32 = mybir.dt.uint32
U16 = mybir.dt.uint16
U8 = mybir.dt.uint8
E4M3 = mybir.dt.float8_e4m3fn_x4
E5M2 = mybir.dt.float8_e5m2_x4
E2M1 = mybir.dt.float4_e2m1fn_x4
MAX = mybir.AluOpType.max
MULT = mybir.AluOpType.mult
COPY = mybir.ActivationFunctionType.Copy

P = 128
PACK = 4
K_PASS = P * PACK
PASSES = K // K_PASS
HALF = J // 2
N_TILES = N // P
LIST_COLS = HALF // 16
XA, XB = 0, 1
W_SPLIT = 64


def tile_list_joined_rival_floored_kernel(
    tc, xa, xb, w, sx_words, sx_scales, ws_words, ws_scales, wb_words, wb_scales, tz, rw, offs, offs2, offs3, out
):
    nc = tc.nc
    with ExitStack() as ctx:
        lists = ctx.enter_context(tc.tile_pool(name="lists", bufs=1))
        sb = ctx.enter_context(tc.tile_pool(name="sb", bufs=1))
        ps = ctx.enter_context(tc.psum_pool(name="ps", bufs=1))

        def tile(name, shape, dtype, tag=None):
            return sb.tile(shape, dtype, name=name, tag=tag or name, align_bytes=64)

        def pass_rows(table, a):
            return table[a * K_PASS : (a + 1) * K_PASS, :].rearrange("(p i) c -> p i c", i=PACK)

        def load_planes(name, table, a, first, count):
            raw = tile(name, [P, count, table.shape[1]], F32)
            nc.sync.dma_start(out=raw[:], in_=pass_rows(table, a)[:, first : first + count, :])
            return [raw[:, i, :] for i in range(count)], raw

        def load_list(name, src):
            dst = lists.tile(list(src.shape), U16, name=name)
            nc.sync.dma_start(dst[:], src)
            return dst

        def load_words(name, src, dtype, width):
            dst = tile(name, [P, width], dtype)
            nc.sync.dma_start(out=dst[:].bitcast(I32), in_=src.bitcast(I32))
            return dst

        staged = tile("staged_scales", [P, 4, R + J + N], U8)
        given_scales = staged[:, 0, :]
        nc.vector.memset(given_scales.bitcast(U32), 0)
        ws_scale_raw = given_scales[:, 0:R]
        sx_scale = given_scales[:, R : R + J]
        wb_scale = given_scales[:, R + J : R + J + N]

        def load_scales(src, first):
            width = src.shape[2]
            nc.sync.dma_start(
                out=staged[0:P:32, :, first : first + width].bitcast(I32),
                in_=src[0].rearrange("(q r) c -> q r c", r=4).bitcast(I32),
            )

        def deal_scales():
            for r in range(1, 4):
                nc.sync.dma_start(out=staged[r:P:32, 0, :].bitcast(I32), in_=staged[0:P:32, r, :].bitcast(I32))

        rw_rows = tile("rw_rows", [P, P], F32)
        nc.vector.memset(rw_rows[:], 0.0)
        ident = tile("ident", [P, P], F32)
        make_identity(nc, ident[:])

        windows = {}
        w_raw = {}
        xb_raw = tile("xb", [P, PASSES, PACK * S], F32)
        nc.sync.dma_start(out=xb_raw[:], in_=xb.rearrange("(a p i) c -> p a (i c)", a=PASSES, i=PACK))
        for a in range(PASSES):
            windows[XB, a] = [xb_raw[:, a, i * S : (i + 1) * S] for i in range(PACK)]
        offsets = {XB: load_list("offs2", offs2)}
        load_scales(ws_scales, 0)
        load_scales(sx_scales, R)
        load_scales(wb_scales, R + J)
        unused, w_raw[0] = load_planes("w0", w, 0, 0, PACK)
        nc.sync.dma_start(out=rw_rows[0:2, :], in_=rw.rearrange("o (h c) -> (o h) c", h=2))
        unused, w_raw[1] = load_planes("w1", w, 1, 0, PACK)
        ws_raw = load_words("ws_raw", ws_words[0].rearrange("p c t -> p (c t)"), U32, R)
        deal_scales()
        sx_rows = sx_words[0].rearrange("p c t -> p (c t)")
        sx_codes = {XB: load_words("sx_codes1", sx_rows[:, PACK * HALF :], U32, HALF)}
        windows[XA, 0], unused = load_planes("xa0", xa, 0, 0, PACK)
        offsets[XA] = load_list("offs", offs)
        first, unused = load_planes("xa1_01", xa, 1, 0, 2)
        sx_codes[XA] = load_words("sx_codes0", sx_rows[:, : PACK * HALF], U32, HALF)
        second, unused = load_planes("xa1_2", xa, 1, 2, 1)
        third, unused = load_planes("xa1_3", xa, 1, 3, 1)
        windows[XA, 1] = first + second + third
        wb_codes = load_words("wb_codes", wb_words[0], U8, 2 * N)
        tz_offsets = load_list("offs3", offs3)
        tz_raw = []
        for nt in range(N_TILES):
            raw = tile("tz%d" % nt, [P, Z], F32)
            nc.sync.dma_start(out=raw[:], in_=tz[nt * P : (nt + 1) * P, :])
            tz_raw.append(raw)

        rw_bank = ps.tile([P, 3, P], F32, name="rw_bank")
        nc.tensor.transpose(rw_bank[:, 2, :], rw_rows[:], ident[:])
        rw_cols = tile("rw_cols", [P, 2], F32)
        nc.scalar.copy(out=rw_cols[:], in_=rw_bank[:, 2, 0:2])
        for h in range(2):
            nc.tensor.transpose(rw_bank[:, h, :], rw_cols[:, h : h + 1].to_broadcast([P, P]), ident[:])
        rw_all = tile("rw_all", [P, 2, P], F32)
        nc.scalar.copy(out=rw_all[:], in_=rw_bank[:, 0:2, :])

        def quantise(name, values, fmt):
            width = values.shape[1] // PACK
            codes = tile(name + "_codes", [P, width], U32)
            scales = tile(name + "_scales", [P, width], U8)
            nc.vector.quantize_mx(out=codes[:].bitcast(fmt), scales=scales[:], in_=values)
            return codes, scales

        def quantise_w(a):
            rounded = tile("w_bf%d" % a, [P, R * PACK], BF16)
            dealt = rounded[:].rearrange("p (t m i) -> p m t i", t=PACK, i=PACK)
            source = w_raw[a][:].rearrange("p i (m t) -> p m t i", t=PACK)
            nc.scalar.copy(out=dealt[:, :W_SPLIT], in_=source[:, :W_SPLIT])
            nc.vector.tensor_copy(out=dealt[:, W_SPLIT:], in_=source[:, W_SPLIT:])
            return quantise("w%d" % a, rounded[:], E5M2)

        def quantise_u(h, a):
            rounded = tile("u_bf%d%d" % (h, a), [P, HALF, PACK], BF16)
            if (h, a) == (XA, 0):
                picked = tile("u_picked", [P, PACK, HALF], F32)
                for i in range(PACK):
                    nc.scalar.activation(picked[:, i, :], windows[h, a][i].indirect(offsets[h][:]), COPY)
                nc.vector.tensor_copy(out=rounded[:], in_=picked[:].rearrange("p i j -> p j i"))
            else:
                for i in range(PACK):
                    nc.vector.tensor_copy(out=rounded[:, :, i], in_=windows[h, a][i].indirect(offsets[h][:]))
            return quantise("u%d%d" % (h, a), rounded[:].rearrange("p j i -> p (j i)"), E4M3)

        a_bank = [ps.tile([P, PACK, HALF], F32, name="a_bank%d" % h) for h in range(2)]

        def first_product(h, a, wq, uq):
            for t in range(PACK):
                cols = slice(t * P, (t + 1) * P)
                nc.tensor.matmul_mx(
                    out=a_bank[h][:, t, :],
                    lhsT=wq[0][:, cols].bitcast(E5M2),
                    lhsT_scale=wq[1][:, cols],
                    rhs=uq[0][:].bitcast(E4M3),
                    rhs_scale=uq[1][:],
                    start=(a == 0 and t == 0),
                    stop=(a == PASSES - 1 and t == PACK - 1),
                )

        def rival(h, ws_codes, ws_scale):
            bank = ps.tile([P, PACK, HALF], F32, name="b2_bank%d" % h)
            slots = slice(h * HALF, (h + 1) * HALF)
            for t in range(PACK):
                cols = slice(t * P, (t + 1) * P)
                nc.tensor.matmul_mx(
                    out=bank[:, t, :],
                    lhsT=ws_codes[:, cols].bitcast(E5M2),
                    lhsT_scale=ws_scale[:, cols],
                    rhs=sx_codes[h][:].bitcast(E5M2),
                    rhs_scale=sx_scale[:, slots],
                    start=True,
                    stop=True,
                )
            b2 = tile("b2_%d" % h, [P, HALF, PACK], F32)
            nc.scalar.copy(out=b2[:], in_=bank[:].rearrange("p t j -> p j t"))
            return b2

        def larger(h, b2):
            hid = tile("hid%d" % h, [P, HALF, PACK], BF16)
            nc.vector.tensor_tensor(out=hid[:], in0=a_bank[h][:].rearrange("p t j -> p j t"), in1=b2[:], op=MAX)
            return quantise("hid%d" % h, hid[:].rearrange("p j t -> p (j t)"), E5M2)

        def second_product(hid, banks):
            codes, scales = hid
            for nt in range(N_TILES):
                nc.tensor.matmul_mx(
                    out=banks[nt],
                    lhsT=wb_codes[:, 2 * nt * P : 2 * (nt + 1) * P].bitcast(E2M1),
                    lhsT_scale=wb_scale[:, nt * P : (nt + 1) * P],
                    rhs=codes[:].bitcast(E5M2),
                    rhs_scale=scales[:],
                    start=True,
                    stop=True,
                )

        def gather_tz(h):
            picked = tile("tz_picked%d" % h, [P, N_TILES, HALF], F32, tag="picked_then_floored" if h == XB else None)
            cols = tz_offsets[:, h * LIST_COLS : (h + 1) * LIST_COLS]
            for nt in range(N_TILES):
                nc.scalar.activation(picked[:, nt, :], tz_raw[nt][:].indirect(cols), COPY)
            return picked

        p_xb = ps.tile([P, N_TILES, HALF], F32, name="p_xb")
        p_xa = [ps.tile([P, HALF], F32, name="p_xa%d" % nt) for nt in range(N_TILES)]
        p_banks = {XB: [p_xb[:, nt, :] for nt in range(N_TILES)], XA: [b[:] for b in p_xa]}

        wq = {}
        uq0 = quantise_u(XB, 0)
        uq = quantise_u(XB, 1)
        wq[0] = quantise_w(0)
        first_product(XB, 0, wq[0], uq0)
        ws_codes = tile("ws_codes", [P, R], U32)
        ws_scale = tile("ws_scale", [P, R], U8)
        nc.vector.tensor_copy(
            out=ws_scale[:].rearrange("p (t m) -> p t m", t=PACK), in_=ws_scale_raw.rearrange("p (m t) -> p t m", t=PACK)
        )
        nc.vector.tensor_copy(
            out=ws_codes[:].rearrange("p (t m) -> p t m", t=PACK), in_=ws_raw[:].rearrange("p (m t) -> p t m", t=PACK)
        )
        wq[1] = quantise_w(1)
        b2 = {XB: rival(XB, ws_codes, ws_scale)}
        first_product(XB, 1, wq[1], uq)
        hid_xb = larger(XB, b2[XB])
        first_product(XA, 0, wq[0], quantise_u(XA, 0))
        b2[XA] = rival(XA, ws_codes, ws_scale)
        second_product(hid_xb, p_banks[XB])
        first_product(XA, 1, wq[1], quantise_u(XA, 1))
        picked = {h: gather_tz(h) for h in (XB, XA)}
        second_product(larger(XA, b2[XA]), p_banks[XA])
        out_tiles = out.rearrange("(nt p) (h j) -> p nt h j", p=P, j=HALF)

        floored = tile("floored_xb", [P, N_TILES, HALF], F32)
        nc.vector.tensor_tensor(out=floored[:], in0=p_xb[:], in1=picked[XB][:], op=MAX)
        y = tile("y_xb", [P, N_TILES, HALF], F32)
        weights = rw_all[:, XB : XB + 1, :].to_broadcast([P, N_TILES, HALF])
        nc.vector.tensor_tensor(out=y[:], in0=floored[:], in1=weights, op=MULT)
        nc.sync.dma_start(out=out_tiles[:, :, XB, :], in_=y[:])

        floored = tile("floored_xa", [P, N_TILES, HALF], F32, tag="picked_then_floored")
        for nt in range(N_TILES):
            nc.vector.tensor_tensor(out=floored[:, nt, :], in0=p_banks[XA][nt], in1=picked[XA][:, nt, :], op=MAX)
        for nt, queue in enumerate((nc.sync, nc.scalar)):
            y = tile("y_xa%d" % nt, [P, HALF], F32)
            nc.vector.tensor_tensor(out=y[:], in0=floored[:, nt, :], in1=rw_all[:, XA, :], op=MULT)
            queue.dma_start(out=out_tiles[:, nt, XA, :], in_=y[:])
